import numpy as np
import ml_dtypes

BF16 = ml_dtypes.bfloat16


def bf(x):
    return np.asarray(x, np.float32).astype(BF16)


def f32(x):
    return np.asarray(x, np.float32)


def f64(x):
    return np.asarray(x).astype(np.float64)


def striped(idx):
    return np.tile(idx.reshape(-1, 16).T, (8, 1))


S, K, M, N, E, Q = 512, 256, 512, 192, 2, 96


def setup_inputs():
    return {"base": bf(np.random.standard_normal((M, S))), "x": bf(np.random.standard_normal((K, N))), "w": bf(np.random.standard_normal((E, K, M)) / np.sqrt(K)), "offs": striped(np.random.permutation(S)[:N])}


def reference(base, x, w, offs):
    idx = offs[:16].T.reshape(-1)
    z = f64(base).copy()
    for e in range(E):
        z[:, idx[e * Q : (e + 1) * Q]] += f64(w)[e].T @ f64(x)[:, e * Q : (e + 1) * Q]
    return z

@@ -1,0 +1,74 @@
+import concourse.mybir as mybir
+from concourse.masks import make_identity
+
+BF16, F32, U16 = mybir.dt.bfloat16, mybir.dt.float32, mybir.dt.uint16
+
+P = 128
+TOKENS = 512
+FEATURES = 512
+CONTRACT = 256
+ENTRIES = 192
+EXPERTS = 2
+PIECE = ENTRIES // EXPERTS
+PIECE_COLS = PIECE // 16
+ROW_BLOCKS = FEATURES // P
+K_BLOCKS = CONTRACT // P
+
+FLOPS = 2 * CONTRACT * FEATURES * ENTRIES
+
+
+def tile_scatter_matmul_kernel(tc, base, x, w, offs, out):
+    nc = tc.nc
+    with (
+        tc.tile_pool(name="held", bufs=1) as held,
+        tc.psum_pool(name="windows", bufs=1) as windows,
+    ):
+        offsets = held.tile([P, ENTRIES // 16], U16, name="offsets")
+        nc.sync.dma_start(offsets[:], offs)
+
+        ident = held.tile([P, P], BF16, name="ident")
+        make_identity(nc, ident[:])
+
+        queues = (nc.sync, nc.scalar)
+        base_tiles = []
+        for r in range(ROW_BLOCKS):
+            base_tile = held.tile([P, TOKENS], BF16, name="base%d" % r)
+            queues[r % 2].dma_start(base_tile[:], base[r * P : (r + 1) * P, :])
+            base_tiles.append(base_tile)
+        x_tiles = []
+        for k in range(K_BLOCKS):
+            x_tile = held.tile([P, ENTRIES], BF16, name="x%d" % k)
+            queues[k % 2].dma_start(x_tile[:], x[k * P : (k + 1) * P, :])
+            x_tiles.append(x_tile)
+        w_tiles = {}
+        for e in range(EXPERTS):
+            for k in range(K_BLOCKS):
+                w_tile = held.tile([P, FEATURES], BF16, name="w%d_%d" % (e, k))
+                queues[k % 2].dma_start(w_tile[:], w[e, k * P : (k + 1) * P, :])
+                w_tiles[(e, k)] = w_tile
+
+        window_tiles = []
+        for r in range(ROW_BLOCKS):
+            window = windows.tile([P, TOKENS], F32, name="window%d" % r)
+            nc.tensor.matmul(window[:], ident[:], base_tiles[r][:], start=True, stop=False)
+            window_tiles.append(window)
+
+        for r in range(ROW_BLOCKS):
+            window = window_tiles[r]
+            for e in range(EXPERTS):
+                piece = offsets[:, e * PIECE_COLS : (e + 1) * PIECE_COLS]
+                for k in range(K_BLOCKS):
+                    nc.tensor.matmul(
+                        window[:].indirect(piece),
+                        w_tiles[(e, k)][:, r * P : (r + 1) * P],
+                        x_tiles[k][:, e * PIECE : (e + 1) * PIECE],
+                        start=False,
+                        stop=(e == EXPERTS - 1 and k == K_BLOCKS - 1),
+                    )
+
+            result = held.tile([P, TOKENS], F32, name="result%d" % r)
+            if r % 2 == 0:
+                nc.vector.tensor_copy(result[:], window[:])
+            else:
+                nc.scalar.copy(result[:], window[:])
+            queues[r % 2].dma_start(out[r * P : (r + 1) * P, :], result[:])

@@ -13,6 +13,7 @@ PIECE = ENTRIES // EXPERTS
 PIECE_COLS = PIECE // 16
 ROW_BLOCKS = FEATURES // P
 K_BLOCKS = CONTRACT // P
+WARMUPS = 3
 
 FLOPS = 2 * CONTRACT * FEATURES * ENTRIES
 
@@ -25,6 +26,12 @@ def tile_scatter_matmul_kernel(tc, base, x, w, offs, out):
     ):
         offsets = held.tile([P, ENTRIES // 16], U16, name="offsets")
         nc.sync.dma_start(offsets[:], offs)
+
+        zeros = held.tile([P, TOKENS], BF16, name="zeros")
+        nc.gpsimd.memset(zeros[:], 0.0)
+        unread = windows.tile([P, TOKENS], F32, name="unread")
+        for i in range(WARMUPS):
+            nc.tensor.matmul(unread[:], zeros[:, 0:P], zeros[:], start=True, stop=True)
 
         ident = held.tile([P, P], BF16, name="ident")
         make_identity(nc, ident[:])

@@ -36,41 +36,41 @@ def tile_scatter_matmul_kernel(tc, base, x, w, offs, out):
         ident = held.tile([P, P], BF16, name="ident")
         make_identity(nc, ident[:])
 
-        queues = (nc.sync, nc.scalar)
-        base_tiles = []
+        base_rows = base.rearrange("(r p) s -> p r s", p=P)
+        base_halves = []
+        for h in range(2):
+            base_half = held.tile([P, 2, TOKENS], BF16, name="base_half%d" % h)
+            nc.sync.dma_start(base_half[:], base_rows[:, 2 * h : 2 * h + 2, :])
+            base_halves.append(base_half)
+        x_tile = held.tile([P, K_BLOCKS, ENTRIES], BF16, name="x_tile")
+        nc.sync.dma_start(x_tile[:], x.rearrange("(p a) j -> p a j", a=K_BLOCKS))
+        w_cuts = {}
         for r in range(ROW_BLOCKS):
-            base_tile = held.tile([P, TOKENS], BF16, name="base%d" % r)
-            queues[r % 2].dma_start(base_tile[:], base[r * P : (r + 1) * P, :])
-            base_tiles.append(base_tile)
-        x_tiles = []
-        for k in range(K_BLOCKS):
-            x_tile = held.tile([P, ENTRIES], BF16, name="x%d" % k)
-            queues[k % 2].dma_start(x_tile[:], x[k * P : (k + 1) * P, :])
-            x_tiles.append(x_tile)
-        w_tiles = {}
-        for e in range(EXPERTS):
-            for k in range(K_BLOCKS):
-                w_tile = held.tile([P, FEATURES], BF16, name="w%d_%d" % (e, k))
-                queues[k % 2].dma_start(w_tile[:], w[e, k * P : (k + 1) * P, :])
-                w_tiles[(e, k)] = w_tile
+            for e in range(EXPERTS):
+                w_cut = held.tile([P, K_BLOCKS, P], BF16, name="w_cut%d_%d" % (r, e))
+                nc.sync.dma_start(
+                    w_cut[:], w[e].rearrange("(p a) m -> p a m", a=K_BLOCKS)[:, :, r * P : (r + 1) * P]
+                )
+                w_cuts[(r, e)] = w_cut
 
         window_tiles = []
         for r in range(ROW_BLOCKS):
             window = windows.tile([P, TOKENS], F32, name="window%d" % r)
-            nc.tensor.matmul(window[:], ident[:], base_tiles[r][:], start=True, stop=False)
+            nc.tensor.matmul(window[:], ident[:], base_halves[r // 2][:, r % 2, :], start=True, stop=False)
             window_tiles.append(window)
 
+        queues = (nc.sync, nc.scalar)
         for r in range(ROW_BLOCKS):
             window = window_tiles[r]
             for e in range(EXPERTS):
                 piece = offsets[:, e * PIECE_COLS : (e + 1) * PIECE_COLS]
-                for k in range(K_BLOCKS):
+                for a in range(K_BLOCKS):
                     nc.tensor.matmul(
                         window[:].indirect(piece),
-                        w_tiles[(e, k)][:, r * P : (r + 1) * P],
-                        x_tiles[k][:, e * PIECE : (e + 1) * PIECE],
+                        w_cuts[(r, e)][:, a, :],
+                        x_tile[:, a, e * PIECE : (e + 1) * PIECE],
                         start=False,
-                        stop=(e == EXPERTS - 1 and k == K_BLOCKS - 1),
+                        stop=(e == EXPERTS - 1 and a == K_BLOCKS - 1),
                     )
 
             result = held.tile([P, TOKENS], F32, name="result%d" % r)

@@ -74,8 +74,5 @@ def tile_scatter_matmul_kernel(tc, base, x, w, offs, out):
                     )
 
             result = held.tile([P, TOKENS], F32, name="result%d" % r)
-            if r % 2 == 0:
-                nc.vector.tensor_copy(result[:], window[:])
-            else:
-                nc.scalar.copy(result[:], window[:])
+            nc.vector.tensor_copy(result[:], window[:])
             queues[r % 2].dma_start(out[r * P : (r + 1) * P, :], result[:])

@@ -59,7 +59,6 @@ def tile_scatter_matmul_kernel(tc, base, x, w, offs, out):
             nc.tensor.matmul(window[:], ident[:], base_halves[r // 2][:, r % 2, :], start=True, stop=False)
             window_tiles.append(window)
 
-        queues = (nc.sync, nc.scalar)
         for r in range(ROW_BLOCKS):
             window = window_tiles[r]
             for e in range(EXPERTS):
@@ -75,4 +74,4 @@ def tile_scatter_matmul_kernel(tc, base, x, w, offs, out):
 
             result = held.tile([P, TOKENS], F32, name="result%d" % r)
             nc.vector.tensor_copy(result[:], window[:])
-            queues[r % 2].dma_start(out[r * P : (r + 1) * P, :], result[:])
+            nc.scalar.dma_start(out[r * P : (r + 1) * P, :], result[:])

@@ -14,6 +14,7 @@ PIECE_COLS = PIECE // 16
 ROW_BLOCKS = FEATURES // P
 K_BLOCKS = CONTRACT // P
 WARMUPS = 3
+BURST = 256
 
 FLOPS = 2 * CONTRACT * FEATURES * ENTRIES
 
@@ -39,15 +40,15 @@ def tile_scatter_matmul_kernel(tc, base, x, w, offs, out):
         base_rows = base.rearrange("(r p) s -> p r s", p=P)
         base_halves = []
         for h in range(2):
-            base_half = held.tile([P, 2, TOKENS], BF16, name="base_half%d" % h)
+            base_half = held.tile([P, 2, TOKENS], BF16, name="base_half%d" % h, align_bytes=BURST)
             nc.sync.dma_start(base_half[:], base_rows[:, 2 * h : 2 * h + 2, :])
             base_halves.append(base_half)
-        x_tile = held.tile([P, K_BLOCKS, ENTRIES], BF16, name="x_tile")
+        x_tile = held.tile([P, K_BLOCKS, ENTRIES], BF16, name="x_tile", align_bytes=BURST)
         nc.sync.dma_start(x_tile[:], x.rearrange("(p a) j -> p a j", a=K_BLOCKS))
         w_cuts = {}
         for r in range(ROW_BLOCKS):
             for e in range(EXPERTS):
-                w_cut = held.tile([P, K_BLOCKS, P], BF16, name="w_cut%d_%d" % (r, e))
+                w_cut = held.tile([P, K_BLOCKS, P], BF16, name="w_cut%d_%d" % (r, e), align_bytes=BURST)
                 nc.sync.dma_start(
                     w_cut[:], w[e].rearrange("(p a) m -> p a m", a=K_BLOCKS)[:, :, r * P : (r + 1) * P]
                 )
@@ -72,6 +73,6 @@ def tile_scatter_matmul_kernel(tc, base, x, w, offs, out):
                         stop=(e == EXPERTS - 1 and a == K_BLOCKS - 1),
                     )
 
-            result = held.tile([P, TOKENS], F32, name="result%d" % r)
+            result = held.tile([P, TOKENS], F32, name="result%d" % r, align_bytes=BURST)
             nc.vector.tensor_copy(result[:], window[:])
             nc.scalar.dma_start(out[r * P : (r + 1) * P, :], result[:])

@@ -14,7 +14,7 @@ PIECE_COLS = PIECE // 16
 ROW_BLOCKS = FEATURES // P
 K_BLOCKS = CONTRACT // P
 WARMUPS = 3
-BURST = 256
+BURST = 2048
 
 FLOPS = 2 * CONTRACT * FEATURES * ENTRIES
 

import concourse.mybir as mybir
from concourse.masks import make_identity

BF16, F32, U16 = mybir.dt.bfloat16, mybir.dt.float32, mybir.dt.uint16

P = 128
TOKENS = 512
FEATURES = 512
CONTRACT = 256
ENTRIES = 192
EXPERTS = 2
PIECE = ENTRIES // EXPERTS
PIECE_COLS = PIECE // 16
ROW_BLOCKS = FEATURES // P
K_BLOCKS = CONTRACT // P
WARMUPS = 3
BURST = 2048

FLOPS = 2 * CONTRACT * FEATURES * ENTRIES


def tile_scatter_matmul_kernel(tc, base, x, w, offs, out):
    nc = tc.nc
    with (
        tc.tile_pool(name="held", bufs=1) as held,
        tc.psum_pool(name="windows", bufs=1) as windows,
    ):
        offsets = held.tile([P, ENTRIES // 16], U16, name="offsets")
        nc.sync.dma_start(offsets[:], offs)

        zeros = held.tile([P, TOKENS], BF16, name="zeros")
        nc.gpsimd.memset(zeros[:], 0.0)
        unread = windows.tile([P, TOKENS], F32, name="unread")
        for i in range(WARMUPS):
            nc.tensor.matmul(unread[:], zeros[:, 0:P], zeros[:], start=True, stop=True)

        ident = held.tile([P, P], BF16, name="ident")
        make_identity(nc, ident[:])

        base_rows = base.rearrange("(r p) s -> p r s", p=P)
        base_halves = []
        for h in range(2):
            base_half = held.tile([P, 2, TOKENS], BF16, name="base_half%d" % h, align_bytes=BURST)
            nc.sync.dma_start(base_half[:], base_rows[:, 2 * h : 2 * h + 2, :])
            base_halves.append(base_half)
        x_tile = held.tile([P, K_BLOCKS, ENTRIES], BF16, name="x_tile", align_bytes=BURST)
        nc.sync.dma_start(x_tile[:], x.rearrange("(p a) j -> p a j", a=K_BLOCKS))
        w_cuts = {}
        for r in range(ROW_BLOCKS):
            for e in range(EXPERTS):
                w_cut = held.tile([P, K_BLOCKS, P], BF16, name="w_cut%d_%d" % (r, e), align_bytes=BURST)
                nc.sync.dma_start(
                    w_cut[:], w[e].rearrange("(p a) m -> p a m", a=K_BLOCKS)[:, :, r * P : (r + 1) * P]
                )
                w_cuts[(r, e)] = w_cut

        window_tiles = []
        for r in range(ROW_BLOCKS):
            window = windows.tile([P, TOKENS], F32, name="window%d" % r)
            nc.tensor.matmul(window[:], ident[:], base_halves[r // 2][:, r % 2, :], start=True, stop=False)
            window_tiles.append(window)

        for r in range(ROW_BLOCKS):
            window = window_tiles[r]
            for e in range(EXPERTS):
                piece = offsets[:, e * PIECE_COLS : (e + 1) * PIECE_COLS]
                for a in range(K_BLOCKS):
                    nc.tensor.matmul(
                        window[:].indirect(piece),
                        w_cuts[(r, e)][:, a, :],
                        x_tile[:, a, e * PIECE : (e + 1) * PIECE],
                        start=False,
                        stop=(e == EXPERTS - 1 and a == K_BLOCKS - 1),
                    )

            result = held.tile([P, TOKENS], F32, name="result%d" % r, align_bytes=BURST)
            nc.vector.tensor_copy(result[:], window[:])
            nc.scalar.dma_start(out[r * P : (r + 1) * P, :], result[:])
